import numpy as np, ml_dtypes
CORES = [9,25,41,57]
N = 4
BF = ml_dtypes.bfloat16
def gentries(a):
    return np.ascontiguousarray(a.reshape(8, 16, -1).transpose(0, 2, 1)).reshape(8, -1)
def gtable(e):
    e = np.asarray(e); return np.ascontiguousarray(e.reshape(8, -1, 16).transpose(0, 2, 1)).reshape(128, -1).astype(np.int32)
S, V, RO, C = 2, 2048, 4, 15
def pairs(rng, F):
    o = np.argsort(rng.random((N, 8, RO, S, V)), axis=-1)
    w = np.ascontiguousarray(o.reshape(N, 8, RO, S, V // 2, 2)[..., ::-1]).reshape(N, 8, RO, S, V)
    w[..., :F] = o[..., :F]
    m = np.empty_like(o); np.put_along_axis(m, o, w, -1)
    return m
def whole_in(rng, size):
    return np.rint(size * (2.0 * rng.random((N, 8, 16, S, V)) - 1.0)).astype(np.int64)
def parts(rng):
    x = whole_in(rng, rng.choice(np.array([3.0, 10.0, 30.0, 60.0]), (N, 8, 1, S, V)))
    p = np.argsort(rng.random((N, 8, S, V)), axis=-1)
    return x, p, pairs(rng, 2 * (V // 64))
def pack(x, p, m):
    return {"x": np.ascontiguousarray(x.reshape(N, 128, S * V)).astype(np.float32).astype(BF),
            "p": np.stack([gtable(a.reshape(8, -1)) for a in p]), "mate": np.stack([gtable(a.reshape(8, -1)) for a in m])}
def put(x, p, m, g, xs, ps, ms):
    x[:, g] = xs.reshape(N, S, 16, V).transpose(0, 2, 1, 3)
    p[:, g] = ps.reshape(N, S, V)
    m[:, g, :len(ms)] = np.reshape(ms, (-1, N, S, V)).transpose(1, 0, 2, 3)
def sides(rng):
    Z = N * S; h = V // 2
    o = np.argsort(rng.random((Z, V)), axis=-1)
    b = np.empty((Z, V), np.int64); ps = np.empty((Z, V), np.int64); ms = np.empty((Z, V), np.int64)
    np.put_along_axis(b, o, np.tile(np.where(np.arange(V) < h, 1, -1), (Z, 1)), 1)
    np.put_along_axis(ps, o, np.roll(o, -1, axis=0), 1)
    a = o[:, :h]; c = np.take_along_axis(o[:, h:], np.argsort(rng.random((Z, h)), axis=-1), 1)
    np.put_along_axis(ms, a, c, 1); np.put_along_axis(ms, c, a, 1)
    return b, ps, ms
def link(x, p, back, used, mt, z, a, e):
    b = back[z, e]; u = (z + 1) % (N * S)
    if used[z, a] or used[z, b]: return False
    if a != b:
        i = p[z, a]
        va, vb, vi, ve = x[z, :, a], x[z, :, b], x[u, :, i], x[u, :, e]
        if np.sum(np.abs(va - vi) + np.abs(vb - ve) - np.abs(va - ve) - np.abs(vb - vi)) <= 0: return False
        mt[z, a] = b; mt[z, b] = a
    used[z, a] = True; used[z, b] = True
    return True
def grow(rng):
    Z = N * S; h = C // 2
    x = rng.integers(-60, 61, (Z, 16, V))
    x[:, :4] = np.where(rng.random((Z, 1, V)) < 0.0625, 60 - h, 60) * np.array([1, 1, -1, 1])[None, :, None]
    p = np.argsort(rng.random((Z, V)), axis=-1); m = np.tile(np.arange(V), (RO, Z, 1)); x0 = x; p0 = p
    for t in range(RO):
        if t > 0:
            back = np.argsort(p, axis=-1); used = np.zeros((Z, V), bool); w = x[:, 0]; hi = 60 + t * h; want = 32 >> (t - 1)
            hot = [np.flatnonzero(w[z] == hi) for z in range(Z)]
            for z in range(Z):
                l = (z - 1) % Z; u = (z + 1) % Z
                for c in rng.permutation(np.flatnonzero(w[z] == hi - h))[:want]:
                    if any(link(x, p, back, used, m[t], l, e, c) for e in rng.permutation(hot[l])[:16]):
                        any(link(x, p, back, used, m[t], z, c, e) for e in rng.permutation(hot[u])[:16])
                if t < RO - 1:
                    for c in rng.permutation(np.flatnonzero((w[z] == 60) & (w[u][p[z]] >= 60) & ~used[z]))[:want]:
                        if not used[z, c] and any(link(x, p, back, used, m[t], l, e, c) for e in rng.permutation(hot[l])[:16]): used[z, c] = True
        p = np.take_along_axis(p, m[t], 1)
        succ = np.take_along_axis(np.roll(x, -1, axis=0), p[:, None, :], 2)
        pred = np.roll(np.take_along_axis(x, np.argsort(p, axis=-1)[:, None, :], 2), 1, axis=0)
        x = x + np.clip(pred + succ - 2 * x, -C, C)
    return x0, p0, m
def setup_inputs(rng):
    return pack(*parts(rng))
def setup_inputs_near(rng):
    x, p, m = parts(rng); x = whole_in(rng, 60.0)
    m[:, :, 0] = pairs(rng, 0)[:, :, 0]; m0 = m[:, :, 0]; ar = np.arange(V)
    x = np.take_along_axis(x, np.minimum(ar, m0)[:, :, None], 4)
    co = np.arange(16)[None, None, :, None, None]; late = (ar > m0)[:, :, None]
    for i in range(2):
        x = x + (rng.integers(0, 16, (N, 8, 1, S, V)) == co) * rng.integers(-3, 4, (N, 8, 1, S, V)) * late
    return pack(np.clip(x, -60, 60), p, m)
def setup_inputs_ties(rng):
    x, p, m = parts(rng)
    x = rng.integers(-1, 2, (N, 8, 16, S, V)) * (np.arange(16)[None, :] <= np.arange(8)[:, None])[None, :, :, None, None]
    return pack(x, p, m)
def setup_inputs_still(rng):
    x, p, m = parts(rng); i = np.arange(V)
    p[:, 0] = i; p[:, 1] = V - 1 - i; p[:, 2] = np.roll(i, 1); p[:, 7] = np.roll(i, -1)
    m[:, 0] = i; m[:, 1] = i ^ 1; m[:, 2] = V - 1 - i; m[:, 4] = m[:, 4, :1].copy(); m[:, 5, RO - 1] = i
    x[:, 3] = x[:1, 3, :, :1, :1].copy()
    return pack(x, p, m)
def setup_inputs_ends(rng):
    x, p, m = parts(rng)
    v = rng.choice(np.array([60, 60, 59, 50, 45]), (N, 8, 16, S, V)); x = np.where(rng.random((N, 8, 16, S, V)) < 0.5, v, -v)
    x[:, 0] = v[:, 0]
    x[:, 1] = 60 * (1 - 2 * (np.arange(N * S).reshape(N, 1, S, 1) & 1))
    x[:, 2] = v[:, 2] * (1 - 2 * rng.integers(0, 2, (N, 1, S, V)))
    Z = N * S; turn = (1 - 2 * (np.arange(Z) & 1))[:, None, None]; odd = (np.arange(Z) & 1)[:, None] == 1
    b, ps, ms = sides(rng)
    put(x, p, m, 3, b[:, None, :] * turn * rng.integers(50, 61, (Z, 16, V)), ps, ms[None])
    b, ps, ms = sides(rng)
    put(x, p, m, 4, b[:, None, :] * np.where(np.arange(16)[None, :, None] < 8, turn, 1) * rng.integers(57, 61, (Z, 16, V)), ps, ms[None])
    put(x, p, m, 5, *grow(rng))
    b, ps, ms = sides(rng); dip = (b > 0) == odd
    xs = rng.integers(-2, 3, (Z, 16, V))
    xs[:, :2] = b[:, None, :] * np.where(dip[:, None, :], 60 - C // 2 + rng.integers(0, 3, (Z, 2, V)), 60)
    xs[:, 2:4] = b[:, None, :] * turn * 60
    xs[:, 4] = rng.integers(-6, 7, (Z, V))
    put(x, p, m, 6, xs, ps, np.stack([np.tile(np.arange(V), (Z, 1)), ms]))
    return pack(x, p, m)
def setup_inputs_spread(rng):
    x, p, m = parts(rng)
    x = whole_in(rng, 60.0 * np.exp2(-rng.integers(0, 7, (N, 8, 1, S, V)).astype(np.float64)) * (rng.random((N, 8, 1, S, V)) > 0.0625))
    return pack(x, p, m)
def check_inputs(d):
    bad = []; i = np.arange(V)
    a = np.asarray(d["x"]).astype(np.float64)
    if not (np.all(np.abs(a) <= 60) and np.all(a == np.rint(a))): bad.append("x whole from -60 to 60")
    q = np.stack([gentries(b) for b in d["p"]]).reshape(N, 8, S, V)
    if not np.all(np.sort(q, axis=-1) == i): bad.append("p permutations")
    m = np.stack([gentries(b) for b in d["mate"]]).reshape(N, 8, RO, S, V).astype(np.int64)
    if np.min(m) < 0 or np.max(m) > V - 1: bad.append("range of mate")
    elif not np.all(np.take_along_axis(m, m, -1) == i): bad.append("mate of the mate")
    return bad
def reference(x, p, mate):
    Z = N * S
    X = x.astype(np.float32).astype(np.int32).reshape(N, 8, 16, S, V).transpose(0, 3, 1, 2, 4).reshape(Z, 8, 16, V)
    P = np.stack([gentries(a) for a in p]).astype(np.int64).reshape(N, 8, S, V).transpose(0, 2, 1, 3).reshape(Z, 8, V)
    M = np.stack([gentries(a) for a in mate]).astype(np.int64).reshape(N, 8, RO, S, V).transpose(2, 0, 3, 1, 4).reshape(RO, Z, 8, V)
    for rnd in range(RO):
        m = M[rnd]
        s = np.take_along_axis(np.roll(X, -1, axis=0), P[:, :, None, :], 3)
        t = np.take_along_axis(s, m[:, :, None, :], 3)
        D = np.add.reduce(np.abs(X - s), axis=2) - np.add.reduce(np.abs(X - t), axis=2)
        go = D + np.take_along_axis(D, m, 2) > 0
        P = np.where(go, np.take_along_axis(P, m, 2), P)
        succ = np.where(go[:, :, None, :], t, s)
        back = np.argsort(P, axis=-1)
        pred = np.roll(np.take_along_axis(X, back[:, :, None, :], 3), 1, axis=0)
        X = X + np.clip(pred + succ - 2 * X, -C, C)
    yx = X.reshape(N, S, 8, 16, V).transpose(0, 2, 3, 1, 4).reshape(N, 128, S * V)
    yp = P.reshape(N, S, 8, V).transpose(0, 2, 1, 3).reshape(N, 8, S * V)
    return {"yx": yx.astype(np.float32).astype(BF), "yp": np.stack([gtable(a) for a in yp]).astype(np.float32)}

from concourse.mybir import AluOpType, ActivationFunctionType

V, RO, CL = 2048, 4, 15
HV, QV = 1024, 512
LW = 128 + RO * 256
ALU = AluOpType
ACT = ActivationFunctionType

SCRATCH = {
    "XA": ("sbuf", [128, 5 * V], "bfloat16"), "XB": ("sbuf", [128, 5 * V], "bfloat16"),
    "XP": ("sbuf", [128, 4 * V], "bfloat16"), "XN": ("sbuf", [128, 4 * V], "bfloat16"),
    "SS": ("sbuf", [128, 2 * V], "bfloat16"), "BB": ("sbuf", [128, 2 * V], "bfloat16"),
    "RR": ("sbuf", [128, 2 * V], "bfloat16"), "WW": ("sbuf", [128, 2 * V], "bfloat16"),
    "WM": ("sbuf", [128, 2 * V], "bfloat16"), "EE": ("sbuf", [128, 2 * V], "bfloat16"),
    "FF": ("sbuf", [128, 2 * V], "bfloat16"), "DD": ("sbuf", [128, 2 * V], "bfloat16"),
    "YY": ("sbuf", [128, V], "bfloat16"),
    "PI": ("sbuf", [128, 256], "int32"), "MI": ("sbuf", [128, 1024], "int32"),
    "MF": ("sbuf", [128, 1024], "float32"), "MH": ("sbuf", [128, 1024], "bfloat16"), "IF": ("sbuf", [128, 128], "float32"),
    "LA": ("sbuf", [128, LW], "uint16"), "LB": ("sbuf", [128, LW], "uint16"), "LP": ("sbuf", [128, LW], "uint16"),
    "PU": ("sbuf", [128, 8 * 128], "uint16"), "PB": ("sbuf", [128, 4 * 128], "uint16"),
    "PF": ("sbuf", [128, 11 * 128], "float32"), "PH": ("sbuf", [128, 8 * 256], "bfloat16"),
    "HL": ("sbuf", [128, 8 * 256], "bfloat16"), "GO": ("sbuf", [128, 256], "float32"), "GD": ("sbuf", [128, 256], "float32"),
    "IZ": ("sbuf", [128, 144], "float32"), "ID": ("sbuf", [128, 128], "float32"), "AZ": ("sbuf", [128, 3 * 144], "float32"),
    "ZZ": ("sbuf", [128, 4 * 144], "bfloat16"), "II": ("sbuf", [128, 5 * 128], "bfloat16"),
    "ps": ("psum", [128, 4096], "float32"),
}
SEMAPHORES = (["pe", "ve", "ac", "gp", "sent", "st", "lq"]
              + ["ld%d" % i for i in range(7)]
              + ["w%s%s%d" % (k, d, t) for k in "HP" for d in "pa" for t in range(RO)]
              + ["%s%d%d" % (k, t, j) for k in ("xp", "xh", "xn") for t in range(RO) for j in range(2)]
              + ["pb%d" % t for t in range(RO)] + ["lp%d" % t for t in range(RO)])

PLAN = "ph=a;Hh=va;Sp=aavv;Sa=aaaa;Mp=aaaa;Ma=aaav;Ap=aa;Aa=aa;Fp=4;Fa=4;Cp=w;Ca=h;Ea=aaaa;Eb=aaaa;fa=aaaa;fb=aaaa;U=ba;D=ap;pl=a;la=vvvv;lb=vvvv;Sa.0=aava;bk=D;Fa.1=2;Sp.1=aava;Ap.1=va;Sa.1=avav;Fa.2=2;Sa.3=aaav;Fp.0=2;fa.2=aaav;fa.3=aavv;lb.2=aaav;lb.3=aaav;Aa.2=va;Fp.1=2;fb.2=aaav;Ca.2=w;Ma.3=avaa;Aa.0=vv;Ma.0=avaa;fb.0=vvvv;Eb.1=aavv;lb.1=aaav;fa.0=aaav;la.3=vava;fb.3=aaav;Sp.2=vava;Fp.3=2;Ma.1=aaaa;Sp.0=aaaa;la.0=vava;Fp.2=2;lb.0=vvaa"
ORDER = "AAABACADAHAIAEAFAJAKALAWAXAZAQAbARASAUAMBBBPBCBQBRBSBTBUBVBWAcAdAYAVATANBYAaBXAeAfBFBABaBZBeCABHAGBIBbBDBECUCVBfBcAPBGAOBJDVCBBdCYCCBLCZCWCDCcDECXBKCECaBMCbDABNDBCeCfCdDCDDDFCFBOCHDXCGCICJDGDHDWDYCKDICOCLCPCMCNCQEIDZDJDKCRDMDLDODNFACSEJDeCTDaEKDPELDQDRDSDbFCFBDfEAEBEMEPENEODTDUECEDEEEGEHETEQEFEbEYFQFKFDEUEREZFFFNFEFIFGEVESFJEcEaEdFOFPFRDcDdFVEWEXFLFHFaFSFMFXFWFbGAGCFcEeEfFfGBGHFYGDFZGFGEGGFTFUFdFeGJGRGLGNGMGOGIGPHEGQGKGSGTHGHHGUHFHJGVHIHNHOHLHMHPHKHQHRGWHSIEIFGXHTHUGZGYIGHVGaICIDGbGeGfGcGdIHHWHXJWHAIIHBHYHZHaHbIVHcHCHdHDHeHfIJIKILIPJXIWIAIBIMIQIRISIaIXIUJYIeIYINITIbJBIZJEIcJCIdIOJPJJIfJQJKJDJLJFJGJAJaJRJSJTJHJIJZJMJNJcJOJUJVKXKWJbJdKAKFJeJfKKKDKBKPKEKCKLKGKHKMKQKNKIKJKOKRKSKTKYKaKcKUKVLCKdKZKeLAKfKbLBLVLTLDLUMALYLeLELFLSLWLaMCLZLcMELGLJLfLXLbMBLdMDLHMFLIMGLLLKLMMHLNMIMWMXMYMZLOMVLPLQMeMJLRNIMKMLMMMNMOOIMPMQMRMfNAOHNBNXMSNCNDNENFNRMTMUNGNHNJOJNKNONLNUNNOCODOKNPNVNQOLNMNSNcNWNYNTNdNZNeNaNbOMNfONOOOAOBOPOUPAObOROEMaOQPFOFOGOSOTOVMbPBOcPHPCMcMdOWOXOYPGOZOaOdPIPKOePMPSPJOfPQPLPTPRPDPEPOPWPUPNPPPVPXQKQLQMPYPZPaQaQSQWQUQXQVQOQYQQQZQNQPQbQRQTPbPcPePfPdQcQdQeQAQEQBQFQCQDQfQGRQRARBQHRCRDQIRRQJRSRFRERGSSSRRMRHRIRJRKRTRURORPRbRXRYRZSTRVRWSUSGRfSNSOSCSVSHRaSARcRdSISXSBSWSJReSKSDSfSZSYTKSLSESFSbTCSMSPSaTATBSQScTGSdSeRLTLTMTHTNTITDTERNTFTJ"
BANKS = dict(A=(6, 6, 4, 4), B=(4, 4, 4, 4), C=(4, 6, 4, 4), D=(6, 4, 4, 4))


def plan_cfg(text):
    P = dict(kv.split("=") for kv in text.split(";"))
    e = {"a": "ac", "v": "ve"}

    def split(code):
        out = []
        for q, ch in enumerate(code):
            if out and q != 2 and out[-1][2] == e[ch]:
                out[-1] = (out[-1][0], (q + 1) * QV, e[ch])
            else:
                out.append((q * QV, (q + 1) * QV, e[ch]))
        return out

    c = {"ph": e[P["ph"]], "pl": e[P["pl"]], ("Hh", "p"): e[P["Hh"][0]], ("Hh", "a"): e[P["Hh"][1]], "bk": BANKS[P["bk"]]}
    for t in range(RO):
        f = lambda k: P.get("%s.%d" % (k, t), P[k])
        for d in "pa":
            n = int(f("F" + d))
            c["S", d, t], c["M", d, t], c["A", d, t] = split(f("S" + d)), split(f("M" + d)), [e[x] for x in f("A" + d)]
            c["F", d, t] = [(i * V // n, (i + 1) * V // n, "ve") for i in range(n)]
            c["C", d, t] = {"w": "whole", "h": "half"}[f("C" + d)]
        for z in "ab":
            c["E", z, t], c["fin", z, t], c["cl", z, t] = split(f("E" + z)), [e[x] for x in f("f" + z)], [e[x] for x in f("l" + z)]
        c["U", t], c["D", t] = f("U"), f("D")
    return c


def order_of(text):
    al = "ABCDEFGHIJKLMNOPQRSTUVWXYZabcdef"
    return [al.index(text[i]) * 32 + al.index(text[i + 1]) for i in range(0, len(text), 2)]


def helper_of(core, T, topo):
    return [k for k in topo.cores_of(core) if topo.die(k) != topo.die(core) and T.rank_of(k) is None][0]


def make_ops(g, T, net, cfg):
    ops = []

    def op(name, eng, emit, R, W, cost, sem=None, cnt=1, link=None):
        ops.append(dict(name=name, eng=eng, emit=emit, R=R, W=W, cost=cost, sem=sem or eng, cnt=cnt, link=link))

    def ap(r):
        return T[r[0]][:, r[1]:r[2]]

    def bank(b):
        return ("ps", b, b + 1)

    def ps(b, lo, hi):
        return T.ps[:, b * 512 + lo:b * 512 + hi]

    def sub(r, lo, hi):
        return (r[0], r[1] + lo, r[1] + hi)

    def lst(r, lo, hi):
        return sub(r, lo // 16, hi // 16)

    vec, act, pe = "ve", "ac", "pe"

    def send(name, src, dst, to, sem):
        op(name, "gp", lambda: g.remote_dma(ap(dst), ap(src), T.sem[sem], T.sem.sent, net[to][1], net[to][0], net[to][2]),
           [src], [], ("send", to, (src[2] - src[1]) * 2), sem="sent", cnt=net and net[to][3])

    def recv(name, dst, sem, link):
        op(name, None, None, [], [dst], None, sem=sem, cnt=net and net["nxt"][3], link=link)

    def mms(items):
        def f():
            last = None
            for (o, l, r, s0, s1) in items():
                last = g.tensor.matmul(o, l, r, s0, s1)
            return last
        return f

    def zr(k, r):
        return T.ZZ[:, k * 144 + 15 - r:k * 144 + 143 - r]

    def ii(k):
        return T.II[:, k * 128:(k + 1) * 128]

    Zs = [("ZZ", k * 144, (k + 1) * 144) for k in range(4)]
    Is = [("II", k * 128, (k + 1) * 128) for k in range(5)]

    def strided(o, k, src, first, last):
        return [(o, zr(k, r), T[src[0]][:, src[1] + r:src[2]:16], first and r == 0, last and r == 15) for r in range(16)]

    def gather(name, eng, out, win, offs, extra=()):
        if eng == vec:
            f = lambda: g.vector.tensor_copy(ap(out), ap(win).indirect(ap(offs)))
        else:
            f = lambda: g.scalar.activation(ap(out), ap(win).indirect(ap(offs)), ACT.Copy)
        op(name, eng, f, [win, offs] + list(extra), [out], ("gather", out[2] - out[1]))

    def acopy(name, out, src, R, W):
        op(name, act, lambda: g.scalar.activation(ap(out), src(), ACT.Copy), R, W + [out], ("e", out[2] - out[1], 1.0))

    def tt(name, out, a, b, alu, cost):
        op(name, vec, lambda: g.vector.tensor_tensor(ap(out), ap(a), ap(b), alu), [a, b], [out], cost)

    X = lambda b, t: (b, t * V, (t + 1) * V)
    di = {"p": 0, "a": 1}
    zi = {"a": 0, "b": 1}

    def load(name, q, dst, src, sem, nbytes):
        Q = {"sy": lambda: g.sync, "ac": lambda: g.scalar}[q]
        op(name, q, lambda: Q().dma_start(ap(dst), src()), [], [dst], ("dma", nbytes), sem=sem, cnt=16)

    load("ldp", "ac", ("PI", 0, 256), lambda: T.p[:, :], "ld0", 1024)
    load("ldm0", "ac", ("MI", 0, 256), lambda: T.mate[:, 0:256], "ld1", 1024)
    for j in range(2):
        load("ldb%d" % j, "sy", sub(X("XB", 0), j * HV, (j + 1) * HV), lambda j=j: T.x[:, V + j * HV:V + (j + 1) * HV], "ld%d" % (2 + j), 2048)
    for j in range(2):
        load("lda%d" % j, "sy", sub(X("XA", 0), j * HV, (j + 1) * HV), lambda j=j: T.x[:, j * HV:(j + 1) * HV], "ld%d" % (4 + j), 2048)
    load("ldm1", "sy", ("MI", 256, 1024), lambda: T.mate[:, 256:1024], "ld6", 3072)

    op("ioz", "gp", lambda: g.iota(T.IZ[:, :], [[-16, 9], [-1000, 16]], 15000, 1, allow_small_or_imprecise_dtypes=True),
       [], [("IZ", 0, 144)], ("iota", 144))
    op("iod", "gp", lambda: g.iota(T.ID[:, :], [[1, 128]], 0, -1, allow_small_or_imprecise_dtypes=True),
       [], [("ID", 0, 128)], ("iota", 128))
    for k, cen in enumerate((7.5, 0.5, 2.5)):
        r = ("AZ", k * 144, (k + 1) * 144)
        op("az%d" % k, act, lambda r=r, cen=cen: g.scalar.activation(ap(r), T.IZ[:, :], ACT.Abs, bias=-cen),
           [("IZ", 0, 144)], [r], ("e", 144, 1.0))
    for k, (a, lim, sg) in enumerate(((0, 8.0, 1.0), (0, 8.0, -1.0), (1, 1.0, 1.0), (2, 1.0, 1.0))):
        r = ("AZ", a * 144, (a + 1) * 144)
        op("zz%d" % k, vec, lambda k=k, r=r, lim=lim, sg=sg: g.vector.tensor_scalar(ap(Zs[k]), ap(r), lim, sg, ALU.is_lt, ALU.mult),
           [r], [Zs[k]], ("e", 144, 1.0))
    for k, sg in enumerate((1.0, -1.0, -2.0, -16.0, 1.0 / 128)):
        op("ii%d" % k, vec, lambda k=k, sg=sg: g.vector.tensor_scalar(ap(Is[k]), T.ID[:, :], 0.0, sg, ALU.is_equal, ALU.mult),
           [("ID", 0, 128)], [Is[k]], ("e", 128, 1.0))
    IF = ("IF", 0, 128)
    op("if", vec, lambda: g.vector.tensor_scalar(ap(IF), T.ID[:, :], 0.0, None, ALU.is_equal), [("ID", 0, 128)], [IF], ("e", 128, 1.0))
    for d in "ap":
        r = X("WW", di[d])
        op("wz" + d, vec, lambda r=r: g.vector.memset(ap(r), 0.0), [], [("WH" + d, 0, 1), ("WP" + d, 0, 1)], ("e", V, 0.5))

    def copy(name, out, in_):
        op(name, vec, lambda: g.vector.tensor_copy(ap(out), ap(in_)), [in_], [out], ("e", out[2] - out[1], 1.0))

    copy("pua", ("LA", 0, 128), ("PI", 0, 128))
    copy("pub", ("LB", 0, 128), ("PI", 128, 256))

    def mlist(t):
        m = ("MI", t * 256, (t + 1) * 256)
        for s, L in enumerate(("LA", "LB")):
            copy("mu%d%d" % (t, s), (L, 128 + t * 256, 256 + t * 256), sub(m, s * 128, (s + 1) * 128))
        mf, mh = ("MF",) + m[1:], ("MH",) + m[1:]
        bk = cfg["bk"][3]
        copy("m2%d" % t, mf, m)
        op("m3%d" % t, act, lambda: g.scalar.activation(ap(mh), ap(mf), ACT.Identity, bias=128.53125, scale=0.0625),
           [mf], [mh], ("e", 256, 1.0))
        op("m4%d" % t, pe, mms(lambda: [(ps(bk, 0, 256), ap(IF), ap(mf), True, False),
                                        (ps(bk, 0, 256), ii(3), ap(mh), False, False), (ps(bk, 0, 256), ii(4), ap(mh), False, True)]),
           [mf, mh, IF, Is[3], Is[4]], [bank(bk)], ("pe", 6, 256))
        for s, L in enumerate(("LA", "LB")):
            o = (L, 256 + t * 256, 384 + t * 256)
            op("mt%d%d" % (t, s), vec, lambda o=o, s=s: g.vector.tensor_scalar(ap(o), ps(bk, s * 128, (s + 1) * 128), 128.0, 2047.0 * 129, ALU.mult, ALU.add),
               [], [bank(bk), o], ("e", 128, 1.0))
        lo = 256 if t == 0 else 128 + t * 256
        if t == 0:
            send("sq", ("LB", 0, 256), ("LP", 0, 256), "nxt", "lq")
            recv("rq", ("LP", 0, 256), "lq", "sq")
        send("sl%d" % t, ("LB", lo, 384 + t * 256), ("LP", lo, 384 + t * 256), "nxt", "lp%d" % t)
        recv("rl%d" % t, ("LP", lo, 384 + t * 256), "lp%d" % t, "sl%d" % t)

    mlist(0)

    def PU(d, t):
        if t == 0:
            return ("LP" if d == "p" else "LA", 0, 128)
        k = (t - 1) * 2 + di[d]
        return ("PU", k * 128, (k + 1) * 128)

    PF = lambda d, t: ("PF", (t * 2 + di[d]) * 128, (t * 2 + di[d] + 1) * 128)
    PH = lambda d, t: ("PH", (t * 2 + di[d]) * 256, (t * 2 + di[d] + 1) * 256)
    HL = lambda d, t: ("HL", (t * 2 + di[d]) * 256, (t * 2 + di[d] + 1) * 256)
    ML = lambda d, t, k: ("LP" if d == "p" else "LA", 128 + t * 256 + k * 128, 256 + t * 256 + k * 128)

    def rows(name, d, src, row, tag, sem):
        def f():
            w = X("WW", di[d])
            for k in range(2):
                g.sync.dma_start(T.WW[row + k:128:16, w[1]:w[2]], ap(sub(src, k * 128, (k + 1) * 128))).then_inc(T.sem[sem], 16)
            return None
        op(name, "sy", f, [src], [(tag + d, 0, 1)], ("rows",), sem=sem, cnt=32)

    def prow(d, t):
        pf, ph = PF(d, t), PH(d, t)
        hi, lo = sub(ph, 0, 128), sub(ph, 128, 256)
        if cfg["ph"] == vec:
            copy("ph%s%d" % (d, t), hi, pf)
        else:
            acopy("ph%s%d" % (d, t), hi, lambda: ap(pf), [pf], [])
        if cfg["pl"] == vec:
            tt("pl%s%d" % (d, t), lo, pf, hi, ALU.subtract, ("e", 128, 2.0))
        else:
            bk = 6 + di[d]
            op("pk%s%d" % (d, t), pe, mms(lambda: [(ps(bk, 0, 128), ap(IF), ap(pf), True, False), (ps(bk, 0, 128), ii(1), ap(hi), False, True)]),
               [pf, hi, IF, Is[1]], [bank(bk)], ("pe", 5, 128))
            acopy("pl%s%d" % (d, t), lo, lambda: ps(bk, 0, 128), [], [bank(bk)])
        rows("wP%s%d" % (d, t), d, ph, 2, "WP", "wP%s%d" % (d, t))

    def xsend(z, t, j):
        lo, hi = j * HV, (j + 1) * HV
        if z == "b":
            send("sb%d%d" % (t, j), sub(X("XB", t), lo, hi), sub(X("XP", t), lo, hi), "nxt", "xp%d%d" % (t, j))
            recv("rb%d%d" % (t, j), sub(X("XP", t), lo, hi), "xp%d%d" % (t, j), "sb%d%d" % (t, j))
        else:
            send("sa%d%d" % (t, j), sub(X("XA", t), lo, hi), sub(X("XN", t), lo, hi), "hlp", "xh%d%d" % (t, j))
            recv("ra%d%d" % (t, j), sub(X("XN", t), lo, hi), "xn%d%d" % (t, j), "sa%d%d" % (t, j))

    copy("pfa", PF("a", 0), ("PI", 0, 128))
    copy("pfp", PF("p", 0), PU("p", 0))
    for d in "ap":
        prow(d, 0)
    for z in "ba":
        for j in range(2):
            xsend(z, 0, j)

    def decide(d, t):
        n = "%s%d" % (d, t)
        hb = cfg["bk"][1 if d == "a" else 2]
        xl = X("XP" if d == "p" else "XA", t)
        xu = X("XA" if d == "p" else "XB", t)
        s, b, r, w, wm = (X(k, di[d]) for k in ("SS", "BB", "RR", "WW", "WM"))
        for (lo, hi, e) in cfg["S", d, t]:
            gather("S%s_%d" % (n, lo), e, sub(s, lo, hi), xu, lst(PU(d, t), lo, hi))
        for j in range(2):
            lo, hi = j * HV, (j + 1) * HV
            ho = (hb, 448, 512) if j == 0 else (hb + 1, 0, 64)

            def hsum(nm, k, src, first, last, j=j, ho=ho):
                op("%s%s_%d" % (nm, n, j), pe, mms(lambda: strided(ps(*ho), k, src, first, last)), [src, Zs[k]], [bank(hb + j)], ("pe", 16, 64))

            if cfg["A", d, t][j] == act:
                for q in (2 * j, 2 * j + 1):
                    a0, a1 = q * QV, (q + 1) * QV
                    op("Ad%s_%d" % (n, q), pe, mms(lambda q=q, a0=a0, a1=a1: [
                        (ps(q, 0, 512), ii(1), ap(sub(xl, a0, a1)), True, False), (ps(q, 0, 512), ii(0), ap(sub(s, a0, a1)), False, True)]),
                       [sub(xl, a0, a1), sub(s, a0, a1), Is[0], Is[1]], [bank(q)], ("pe", 2, 512))
                    op("R%s_%d" % (n, q), act, lambda q=q, a0=a0, a1=a1: g.scalar.activation(ap(sub(r, a0, a1)), ps(q, 0, 512), ACT.Relu),
                       [], [bank(q), sub(r, a0, a1)], ("e", QV, 1.0))
                hsum("Hx", 0, sub(xl, lo, hi), True, False)
                first = False
            else:
                tt("A%s_%d" % (n, j), sub(r, lo, hi), sub(s, lo, hi), sub(xl, lo, hi), ALU.max, ("tt", HV))
                first = True
            hsum("Hr", 0, sub(r, lo, hi), first, False)
            ml = lst(ML(d, t, 0), lo, hi)
            op("B%s_%d" % (n, j), vec, lambda lo=lo, hi=hi, ml=ml: g.vector.tensor_tensor(ap(sub(b, lo, hi)), ap(s).indirect(ap(ml)), ap(sub(xl, lo, hi)), ALU.max),
               [s, ml, sub(xl, lo, hi)], [sub(b, lo, hi)], ("gather", HV))
            hsum("Hb", 1, sub(b, lo, hi), False, True)
        hl, ph = HL(d, t), PH(d, t)
        if cfg["Hh", d] == vec:
            op("Hh" + n, vec, lambda: g.vector.tensor_copy(ap(sub(hl, 0, 128)), ps(hb, 448, 576)),
               [], [bank(hb), bank(hb + 1), sub(hl, 0, 128)], ("e", 128, 1.0))
        else:
            acopy("Hh" + n, sub(hl, 0, 128), lambda: ps(hb, 448, 576), [], [bank(hb), bank(hb + 1)])
        op("Hl" + n, vec, lambda: g.vector.tensor_tensor(ap(sub(hl, 128, 256)), ps(hb, 448, 576), ap(sub(hl, 0, 128)), ALU.subtract),
           [sub(hl, 0, 128)], [bank(hb), bank(hb + 1), sub(hl, 128, 256)], ("e", 128, 1.0))
        rows("wH" + n, d, hl, 0, "WH", "wH" + n)
        for (lo, hi, e) in cfg["M", d, t]:
            gather("M%s_%d" % (n, lo), e, sub(wm, lo, hi), w, lst(ML(d, t, 1), lo, hi), [("WH" + d, 0, 1), ("WP" + d, 0, 1)])
        whole = cfg["C", d, t] == "whole"
        pf0, pf1, pu1 = PF(d, t), PF(d, t + 1), PU(d, t + 1)
        for j in range(2):
            lo, hi = j * HV, (j + 1) * HV
            c0, c1 = j * 64, (j + 1) * 64
            for nm, bk, own, sg, zk in (("CG", 6, hl, 0, 2), ("CP", 7, ph, 1, 3)):
                def cmm(bk=bk, c0=c0, c1=c1, lo=lo, hi=hi, own=own, sg=sg, zk=zk):
                    o = ps(bk, c0, c1)
                    return ([(o, ii(sg), ap(sub(own, c0, c1)), True, False), (o, ii(sg), ap(sub(own, 128 + c0, 128 + c1)), False, False)]
                            + strided(o, zk, sub(wm, lo, hi), False, True))
                op("%s%s_%d" % (nm, n, j), pe, mms(cmm), [own, sub(wm, lo, hi), Zs[zk], Is[sg]], [bank(bk)], ("pe", 18, 64))
            if whole and j == 0:
                continue
            if whole:
                c0 = 0
            go, gd = ("GO", di[d] * 128 + c0, di[d] * 128 + c1), ("GD", di[d] * 128 + c0, di[d] * 128 + c1)
            k = c1 - c0
            op("go%s_%d" % (n, j), vec, lambda go=go, c0=c0, c1=c1: g.vector.tensor_scalar(ap(go), ps(6, c0, c1), 0.0, None, ALU.is_gt),
               [], [bank(6), go], ("e", k, 1.0))
            op("gd%s_%d" % (n, j), vec, lambda go=go, gd=gd, c0=c0, c1=c1: g.vector.tensor_tensor(ap(gd), ps(7, c0, c1), ap(go), ALU.mult),
               [go], [bank(7), gd], ("e", k, 1.0))
            tt("pn%s_%d" % (n, j), sub(pf1, c0, c1), gd, sub(pf0, c0, c1), ALU.add, ("e", k, 2.0))
            copy("pu%s_%d" % (n, j), sub(pu1, c0, c1), sub(pf1, c0, c1))
        if d == "p":
            send("sp%d" % t, pu1, ("PB", t * 128, (t + 1) * 128), "prv", "pb%d" % t)
            recv("rp%d" % t, ("PB", t * 128, (t + 1) * 128), "pb%d" % t, "sp%d" % t)

    def update(z, t):
        n = "%s%d" % (z, t)
        d = "p" if z == "a" else "a"
        xc, xo = X("XA" if z == "a" else "XB", t), X("XA" if z == "a" else "XB", t + 1)
        xl = X("XP" if z == "a" else "XA", t)
        xu = X("XB" if z == "a" else "XN", t)
        pe_ = PU("a", t + 1) if z == "a" else ("PB", t * 128, (t + 1) * 128)
        e, f, dl = (X(k, zi[z]) for k in ("EE", "FF", "DD"))
        for (lo, hi, en) in cfg["E", z, t]:
            gather("E%s_%d" % (n, lo), en, sub(e, lo, hi), xu, lst(pe_, lo, hi))
        for (lo, hi, en) in cfg["F", d, t]:
            pl = lst(PU(d, t + 1), lo, hi)
            op("F%s_%d" % (n, lo), vec, lambda lo=lo, hi=hi, pl=pl: g.vector.tensor_copy(ap(f).indirect(ap(pl)), ap(sub(xl, lo, hi))),
               [pl, sub(xl, lo, hi)], [f], ("scatter", hi - lo))
        early, late = (e, f) if z == "a" else (f, e)

        def mm(nm, q, bk, terms, first, last):
            a0, a1 = q * QV, (q + 1) * QV
            op("%s%s_%d" % (nm, n, q), pe,
               mms(lambda: [(ps(bk, 0, 512), ii(k), ap(sub(x, a0, a1)), first and i == 0, last and i == len(terms) - 1) for i, (k, x) in enumerate(terms)]),
               [sub(x, a0, a1) for k, x in terms] + [Is[k] for k, x in terms], [bank(bk)], ("pe", len(terms), 512))

        for q in range(4):
            mm("w1", q, q, [(2, xc), (0, early)], True, False)
        for q in range(4):
            a0, a1 = q * QV, (q + 1) * QV
            fb = cfg["bk"][0] + q % 2
            dq, oq = sub(dl, a0, a1), sub(xo, a0, a1)
            mm("w2", q, q, [(0, late)], False, True)
            ca = cfg["cl", z, t][q] == act and cfg["fin", z, t][q] == act
            if not ca:
                op("cl%s_%d" % (n, q), vec, lambda q=q, dq=dq: g.vector.tensor_scalar(ap(dq), ps(q, 0, 512), -float(CL), float(CL), ALU.max, ALU.min),
                   [], [bank(q), dq], ("e", QV, 1.0))
            else:
                y = ("YY", a0, a1)
                op("ck%s_%d" % (n, q), act, lambda q=q, y=y: g.scalar.activation(ap(y), ps(q, 0, 512), ACT.Relu, bias=float(CL)),
                   [], [bank(q), y], ("e", QV, 1.0))
                op("cl%s_%d" % (n, q), act, lambda y=y, dq=dq: g.scalar.activation(ap(dq), ap(y), ACT.Relu, bias=2.0 * CL, scale=-1.0),
                   [y], [dq], ("e", QV, 1.0))
            if cfg["fin", z, t][q] == act:
                mm("f1", q, fb, [(0, xc)], True, False)
                mm("f2", q, fb, [(1 if ca else 0, dl)], False, True)
                op("fi%s_%d" % (n, q), act, lambda fb=fb, oq=oq, ca=ca: g.scalar.activation(ap(oq), ps(fb, 0, 512), ACT.Identity, bias=float(CL) if ca else 0.0),
                   [], [bank(fb), oq], ("e", QV, 1.0))
            else:
                tt("fi%s_%d" % (n, q), oq, dq, sub(xc, a0, a1), ALU.add, ("tt", QV))
            if t + 1 < RO:
                if q % 2 == 1:
                    xsend(z, t + 1, q // 2)
            else:
                y0 = zi[z] * V + a0
                op("y%s_%d" % (z, q), "sy", lambda oq=oq, y0=y0: g.sync.dma_start(T.yx[:, y0:y0 + QV], ap(oq)),
                   [oq], [], ("dma", 1024), sem="st", cnt=16)

    for t in range(RO):
        for d in cfg["D", t]:
            decide(d, t)
        if t + 1 < RO:
            mlist(t + 1)
            for d in cfg["D", t]:
                prow(d, t + 1)
        if t == RO - 1:
            pfb = ("PF", 10 * 128, 11 * 128)
            copy("pfb", pfb, ("PB", t * 128, (t + 1) * 128))
            for s, r in enumerate((PF("a", RO), pfb)):
                op("yp%d" % s, "sy", lambda s=s, r=r: g.sync.dma_start(T.yp[:, s * 128:(s + 1) * 128], ap(r)),
                   [r], [], ("dma", 512), sem="st", cnt=16)
        for z in cfg["U", t]:
            update(z, t)
    return ops


def find_deps(ops):
    seen = {}
    for i, o in enumerate(ops):
        dep = set()
        for kind, regs in (("R", o["R"]), ("W", o["W"])):
            for (b, lo, hi) in regs:
                for (k2, l2, h2, i2) in seen.get(b, []):
                    if l2 < hi and lo < h2 and (kind == "W" or k2 == "W"):
                        dep.add(i2)
        for (b, lo, hi) in o["W"]:
            seen[b] = [e for e in seen.get(b, []) if not (lo <= e[1] and e[2] <= hi)]
        for kind, regs in (("R", o["R"]), ("W", o["W"])):
            for (b, lo, hi) in regs:
                seen.setdefault(b, []).append((kind, lo, hi, i))
        dep.discard(i)
        o["dep"] = sorted(dep)


def emit_all(g, T, ops, order):
    find_deps(ops)
    assert sorted(order) == list(range(len(ops)))
    Q = {"gp": g, "pe": g.tensor, "ve": g.vector, "ac": g.scalar, "sy": g.sync}
    total, waited = {}, {}
    know = {q: {} for q in Q}
    for pos, k in enumerate(order):
        o = ops[k]
        q = o["eng"]
        if q is not None:
            need = {}
            for i in o["dep"]:
                p = ops[i]
                if p["eng"] == "pe" and q == "pe":
                    assert "at" in p
                    continue
                if p["sem"] not in need or p["at"] > need[p["sem"]]["at"]:
                    need[p["sem"]] = p
            for p in sorted(need.values(), key=lambda p: -p["pos"]):
                if know[q].get(p["sem"], 0) >= p["at"]:
                    continue
                Q[q].wait_ge(T.sem[p["sem"]], p["at"])
                waited[p["sem"]] = max(waited.get(p["sem"], 0), p["at"])
                for s, c in p["clock"].items():
                    know[q][s] = max(know[q].get(s, 0), c)
            ins = o["emit"]()
            if o["sem"] != "sent" and ins is not None:
                ins.then_inc(T.sem[o["sem"]], o["cnt"])
        total[o["sem"]] = total.get(o["sem"], 0) + o["cnt"]
        o["at"] = total[o["sem"]]
        o["pos"] = pos
        o["clock"] = dict(know[q]) if q is not None else {}
        o["clock"][o["sem"]] = o["at"]
    for s in sorted(total, key=lambda s: s == "st"):
        if waited.get(s, 0) < total[s]:
            g.wait_ge(T.sem[s], total[s])


def rank_program(g, core, T, topo):
    cores = list(T.cores)
    n = len(cores)
    rank = T.rank_of(core)
    if rank is None:
        for r, c in enumerate(cores):
            if topo.chip(c) == topo.chip(core) and helper_of(c, T, topo) == core:
                dst = cores[(r - 1) % n]
                rid, pid, _ = topo.addr(dst)
                off = topo.mask(c, cores[(r + 1) % n])
                k_in = bin(topo.mask(c, core) & ~off).count("1")
                for t in range(RO):
                    for j in range(2):
                        a = T.XN[:, t * V + j * HV:t * V + (j + 1) * HV]
                        g.wait_ge(T.sem["xh%d%d" % (t, j)], k_in)
                        g.remote_dma(a, a, T.sem["xn%d%d" % (t, j)], T.sem.sent, pid, rid, topo.mask(core, dst))
                g.wait_ge(T.sem.sent, len(topo.engines(core, dst)) * 2 * RO)
        return
    nxt, prv, hlp = cores[(rank + 1) % n], cores[(rank - 1) % n], helper_of(core, T, topo)
    net = {}
    for k, c in (("nxt", nxt), ("prv", prv), ("hlp", hlp)):
        rid, pid, _ = topo.addr(c)
        m = topo.mask(core, c)
        if k == "hlp":
            m &= ~topo.mask(core, nxt)
        net[k] = (rid, pid, m, bin(m).count("1"))
    emit_all(g, T, make_ops(g, T, net, plan_cfg(PLAN)), order_of(ORDER))
